import numpy as np
import ml_dtypes


def mxq(x, axis, fmt="e4m3"):
    dtype, down = {"e4m3": (ml_dtypes.float8_e4m3fn, 7), "e5m2": (ml_dtypes.float8_e5m2, 14)}[fmt]
    v = np.moveaxis(np.asarray(x, np.float32).astype(ml_dtypes.bfloat16).astype(np.float64), axis, -1)
    blocks = v.reshape(v.shape[:-1] + (-1, 32))
    amax = np.abs(blocks).max(-1, keepdims=True)
    byte = np.maximum(np.where(amax > 0, np.frexp(amax)[1] - 1 + 127, 0) - down, 1)
    scale = np.exp2(byte - 127.0)
    codes = (blocks / scale).astype(np.float32).astype(dtype).astype(np.float64)
    return np.moveaxis((codes * scale).reshape(v.shape), -1, axis)


WIDE = False


def mx_kscale(k):
    if not WIDE:
        return np.ones(k)
    levels = np.array([10, -10, 5, -5, 0])
    if k % 512:
        return np.exp2(np.random.permutation(np.resize(levels, k // 32))).repeat(32)
    a = np.empty((k // 512, 16))
    for p in range(k // 512):
        a[p, :8] = np.random.permutation(np.resize(levels, 8))
        for g in range(8):
            far = levels[np.abs(levels - a[p, g]) >= 10]
            a[p, g + 8] = far[np.random.randint(len(far))]
    return np.exp2(a.ravel()).repeat(32)


def f64(x):
    return np.asarray(x).astype(np.float64)


def striped(idx):
    return np.tile(idx.reshape(-1, 16).T, (8, 1)).astype(np.uint16)


def unstriped(offs):
    return offs[:16].T.reshape(-1).astype(np.int64)


E2M1 = np.array([0.0, 0.5, 1.0, 1.5, 2.0, 3.0, 4.0, 6.0, -0.0, -0.5, -1.0, -1.5, -2.0, -3.0, -4.0, -6.0])


def pack_weight(w, fmt):
    k, n = w.shape
    w = f64(np.asarray(w, np.float32).astype(ml_dtypes.bfloat16)).reshape(k // 32, 32, n)
    amax = np.abs(w).max(1)
    if fmt == "e4m3":
        byte = np.frexp(amax)[1] - 1 + 127 - 7
    else:
        mant, ex = np.frexp(amax / 6.0)
        byte = np.where(mant > 0.5, ex, ex - 1) + 127
    byte = np.clip(np.where(amax > 0, byte, 1), 1, 254)
    scaled = (w * np.exp2(127.0 - byte)[:, None, :]).reshape(k, n).astype(np.float32)
    by_word = np.ascontiguousarray(scaled.reshape(k // 512, 128, 4, n).transpose(0, 1, 3, 2))
    if fmt == "e4m3":
        words = by_word.astype(ml_dtypes.float8_e4m3fn).view(np.uint8)
    else:
        c = by_word.astype(ml_dtypes.float4_e2m1fn).view(np.uint8) & 0xF
        words = (c[..., 0::2] | (c[..., 1::2] << 4)).reshape(k // 512, 128, 2 * n)
    return np.ascontiguousarray(words), np.ascontiguousarray(byte.astype(np.uint8).reshape(k // 512, 16, n))


def unpack_weight(words, scales, fmt):
    g, _, n = scales.shape
    words = np.ascontiguousarray(words).reshape(g, 128, n, -1)
    if fmt == "e4m3":
        vals = words.view(ml_dtypes.float8_e4m3fn).astype(np.float64)
    else:
        nib = np.empty((g, 128, n, 4), np.uint8)
        nib[..., 0::2] = words & 0xF
        nib[..., 1::2] = words >> 4
        vals = E2M1[nib]
    vals = vals * np.repeat(np.exp2(scales.astype(np.float64) - 127.0), 8, axis=1)[..., None]
    return vals.transpose(0, 1, 3, 2).reshape(g * 512, n)


def gelu(v):
    return 0.5 * v * (1.0 + np.tanh(np.sqrt(2.0 / np.pi) * (v + 0.044715 * v**3)))


K, T, S, H, T2, P = 1024, 4096, 1024, 1024, 2048, 1024

def setup_inputs():
    n = np.random.standard_normal
    s = mx_kscale(K)[:, None]
    u = mx_kscale(H)[:, None]
    tab_words, tab_scales = pack_weight(n((K, T)) * s, "e4m3")
    w2_words, w2_scales = pack_weight(1.3 * n((H, H)) / np.sqrt(H) / u * u.T, "e2m1")
    return {
        "tab_words": tab_words, "tab_scales": tab_scales,
        "offs": striped(np.random.permutation(T)[:S]),
        "w1": (0.9 * n((K, H)) / np.sqrt(K) / s * u.T).astype(np.float32),
        "base": (0.7 * n((H, S)) * u).astype(np.float32),
        "page0": (n((H, T2)) * u).astype(np.float32),
        "wgs": np.exp(0.3 * n((128, S))).astype(np.float32),
        "offs2": striped(np.random.permutation(T2)[:S]),
        "offs3": striped(np.random.permutation(T2)[:P]),
        "w2_words": w2_words, "w2_scales": w2_scales,
        "bend": (n(H) / u[:, 0]).astype(np.float32),
        "wgo": np.exp(0.3 * n((128, P))).astype(np.float32),
        "offs4": striped(np.random.permutation(T2)[:P]),
    }

def reference(tab_words, tab_scales, offs, w1, base, page0, wgs, offs2, offs3, w2_words, w2_scales, bend, wgo, offs4):
    v = unpack_weight(tab_words, tab_scales, "e4m3")[:, unstriped(offs)]
    h = (mxq(f64(w1), 0, "e4m3").T @ v) + f64(base)
    page = f64(page0).copy()
    page[:, unstriped(offs2)] = np.tile(f64(wgs), (H // 128, 1)) * h
    x = page[:, unstriped(offs3)]
    w2 = unpack_weight(w2_words, w2_scales, "e2m1")
    d = w2.T @ mxq(np.abs(x), 0, "e4m3")
    y = d * np.tanh(f64(bend)[:, None] * d) + x
    page[:, unstriped(offs4)] = np.tile(f64(wgo), (H // 128, 1)) * y
    return page

@@ -1,0 +1,329 @@
+from contextlib import ExitStack
+
+import concourse.mybir as mybir
+from concourse.masks import make_identity
+
+K, T, S, H, T2 = 1024, 4096, 1024, 1024, 2048
+FLOPS = 2 * K * H * S + 2 * H * H * S
+
+F32 = mybir.dt.float32
+BF16 = mybir.dt.bfloat16
+I32 = mybir.dt.int32
+U32 = mybir.dt.uint32
+U16 = mybir.dt.uint16
+U8 = mybir.dt.uint8
+FP8X4 = mybir.dt.float8_e4m3fn_x4
+FP4X4 = mybir.dt.float4_e2m1fn_x4
+ACT = mybir.ActivationFunctionType
+ADD = mybir.AluOpType.add
+MULT = mybir.AluOpType.mult
+
+P = 128
+PACK = 4
+GROUP = P * PACK
+HALF = 512
+TILES = 8
+
+
+def tile_list_etcher_drift_page_kernel(
+    tc, tab_words, tab_scales, offs, w1, base, page0, wgs, offs2, offs3,
+    w2_words, w2_scales, bend, wgo, offs4, out,
+):
+    nc = tc.nc
+    with ExitStack() as ctx:
+        sb = ctx.enter_context(tc.tile_pool(name="sb", bufs=1))
+        ps = ctx.enter_context(tc.psum_pool(name="ps", bufs=1))
+
+        def sbuf(name, cols, dtype):
+            return sb.tile([P, cols], dtype, name=name, align_bytes=64)
+
+        l_tab = sb.tile([P, S // 16], U16, name="l_tab")
+        l_put1 = sb.tile([P, S // 16], U16, name="l_put1")
+        l_get = sb.tile([P, S // 16], U16, name="l_get")
+        l_put2 = sb.tile([P, S // 16], U16, name="l_put2")
+
+        page = [sbuf("page%d" % i, T2, F32) for i in range(TILES)]
+        hx = [sbuf("hx%d" % b, PACK * S, F32) for b in range(2)]
+        late = sbuf("late", 2 * S, F32)
+        wg = [sbuf("wg%d" % t, S, F32) for t in range(PACK)]
+        tabw = [sbuf("tabw%d" % a, T, U32) for a in range(2)]
+        tabs = sbuf("tabs", T, U8)
+        vw = [[sbuf("vw%d%d" % (a, h), HALF, U32) for h in range(2)] for a in range(2)]
+        vs = [sbuf("vs%d" % h, HALF, U8) for h in range(2)]
+        raw = sbuf("raw", 2 * PACK * GROUP, F32)
+        grouped = [sbuf("grouped%d" % a, PACK * GROUP, BF16) for a in range(2)]
+        codes = [[sbuf("codes%d%d" % (b, a), GROUP, U32) for a in range(2)] for b in range(2)]
+        scales = [[sbuf("scales%d%d" % (b, a), GROUP, U8) for a in range(2)] for b in range(2)]
+        w2raw = sbuf("w2raw", 4 * H, U8)
+        w2p = sbuf("w2p", 4 * H, U8)
+        s2raw = sbuf("s2raw", 2 * H, U8)
+        s2p = sbuf("s2p", 2 * H, U8)
+        stage = [sbuf("stage%d" % n, S, F32) for n in range(2)]
+        ident = sbuf("ident", P, F32)
+        bend_sb = sbuf("bend_sb", TILES, F32)
+
+        mm_banks = [ps.tile([P, HALF], F32, name="mm%d" % n) for n in range(4)]
+        sum_banks = [ps.tile([P, HALF], F32, name="sum%d" % n) for n in range(2)]
+        back_banks = [ps.tile([P, HALF], F32, name="back%d" % n) for n in range(2)]
+
+        def rows(dram, i):
+            b, t = divmod(i, PACK)
+            return dram.rearrange("(b p t) c -> b t p c", b=2, t=PACK)[b, t]
+
+        def listed(lst, c0, n):
+            return lst[:, c0 // 16 : (c0 + n) // 16]
+
+        def h_of(i):
+            b, t = divmod(i, PACK)
+            return late[:, S : 2 * S] if i == TILES - 1 else hx[b][:, t * S : (t + 1) * S]
+
+        def wgs_of(t):
+            return late[:, 0:S] if t == PACK - 1 else wg[t][:]
+
+        def x_planes(b, h):
+            if b == 1 and h == 1:
+                return late[:].rearrange("p (t c) -> p t c", t=PACK)
+            return hx[b][:].rearrange("p (t c) -> p t c", t=PACK)[:, :, h * HALF : (h + 1) * HALF]
+
+        def x_of(i, c0, n):
+            b, t = divmod(i, PACK)
+            h, c = divmod(c0, HALF)
+            if b == 1 and h == 1:
+                return late[:, t * HALF + c : t * HALF + c + n]
+            return hx[b][:, t * S + c0 : t * S + c0 + n]
+
+        def load_dealt(dst, src, t):
+            picked = src.rearrange("(q t) j -> t q j", t=PACK)[t]
+            for c in range(4):
+                nc.sync.dma_start(out=dst[32 * c : 32 * (c + 1), :], in_=picked)
+
+        def load_w1(b, a):
+            src = w1[a * GROUP : (a + 1) * GROUP, b * GROUP : (b + 1) * GROUP]
+            dst = raw[:, a * PACK * GROUP : (a + 1) * PACK * GROUP]
+            nc.sync.dma_start(
+                out=dst.rearrange("p (j c) -> p j c", j=PACK),
+                in_=src.rearrange("(p j) c -> p j c", j=PACK),
+            )
+
+        def load_tab(a):
+            nc.sync.dma_start(
+                out=tabw[a][:].bitcast(I32),
+                in_=tab_words[a].rearrange("p n t -> p (n t)").bitcast(I32),
+            )
+
+        def load_page(i):
+            nc.sync.dma_start(out=page[i][:], in_=rows(page0, i))
+
+        def quantise_w1(b, a):
+            src = raw[:, a * PACK * GROUP : (a + 1) * PACK * GROUP]
+            nc.scalar.copy(
+                out=grouped[a][:].rearrange("p (t m j) -> p m t j", t=PACK, j=PACK),
+                in_=src.rearrange("p (j m t) -> p m t j", j=PACK, t=PACK),
+            )
+            nc.vector.quantize_mx(
+                out=codes[b][a][:].bitcast(FP8X4), scales=scales[b][a][:], in_=grouped[a][:]
+            )
+
+        def add_on_tensor(dst, first, second, turned, step):
+            sum_bank, back_bank = sum_banks[step % 2], back_banks[step % 2]
+            for q in range(HALF // P):
+                blk = slice(q * P, (q + 1) * P)
+                nc.tensor.matmul(sum_bank[:, blk], lhsT=first[:, blk], rhs=ident[:],
+                                 is_transpose=True, start=True, stop=False)
+                nc.tensor.matmul(sum_bank[:, blk], lhsT=second[:, blk], rhs=ident[:],
+                                 is_transpose=True, start=False, stop=True)
+            nc.scalar.copy(out=turned, in_=sum_bank[:])
+            for q in range(HALF // P):
+                blk = slice(q * P, (q + 1) * P)
+                nc.tensor.transpose(back_bank[:, blk], turned[:, blk], ident[:])
+            nc.scalar.copy(out=dst, in_=back_bank[:])
+
+        def make_h(i, h):
+            b, t = divmod(i, PACK)
+            step = 2 * i + h
+            bank = mm_banks[step % 4]
+            cols = slice(t * P, (t + 1) * P)
+            for a in range(2):
+                nc.tensor.matmul_mx(
+                    out=bank[:],
+                    lhsT=codes[b][a][:, cols].bitcast(FP8X4),
+                    lhsT_scale=scales[b][a][:, cols],
+                    rhs=vw[a][h][:].bitcast(FP8X4),
+                    rhs_scale=vs[h][4 * a : P, :],
+                    start=(a == 0),
+                    stop=(a == 1),
+                )
+            dst = h_of(i)[:, h * HALF : (h + 1) * HALF]
+            if i == 0:
+                nc.vector.tensor_tensor(out=dst, in0=bank[:], in1=dst, op=ADD)
+            else:
+                slot = slice((step % 2) * HALF, (step % 2 + 1) * HALF)
+                nc.scalar.copy(out=stage[0][:, slot], in_=bank[:])
+                add_on_tensor(dst, dst, stage[0][:, slot], stage[1][:, slot], step)
+
+        def put_h(i, c0, n):
+            nc.vector.tensor_tensor(
+                out=page[i][:].indirect(listed(l_put1, c0, n)),
+                in0=h_of(i)[:, c0 : c0 + n],
+                in1=wgs_of(i % PACK)[:, c0 : c0 + n],
+                op=MULT,
+            )
+
+        def get_x(i, c0, n):
+            nc.vector.tensor_copy(out=x_of(i, c0, n), in_=page[i][:].indirect(listed(l_get, c0, n)))
+
+        def quantise_abs(b, c0, n):
+            h, c = divmod(c0, HALF)
+            mags = stage[h][:].bitcast(BF16) if b == 0 else grouped[h][:]
+            mags = mags[:, PACK * c : PACK * (c + n)]
+            nc.scalar.activation(
+                out=mags.rearrange("p (c t) -> p c t", t=PACK),
+                in_=x_planes(b, h)[:, :, c : c + n].rearrange("p t c -> p c t"),
+                func=ACT.Abs,
+            )
+            nc.vector.quantize_mx(
+                out=codes[b][h][:, c : c + n].bitcast(FP8X4),
+                scales=scales[b][h][:, c : c + n],
+                in_=mags,
+            )
+
+        def make_product(i, c0, n, step):
+            h, c = divmod(c0, HALF)
+            bank = mm_banks[step % 4][:, 0:n]
+            for a in range(2):
+                col = a * H + i * P
+                nc.tensor.matmul_mx(
+                    out=bank,
+                    lhsT=w2p[:, 2 * col : 2 * (col + P)].bitcast(FP4X4),
+                    lhsT_scale=s2p[:, col : col + P],
+                    rhs=codes[a][h][:, c : c + n].bitcast(FP8X4),
+                    rhs_scale=scales[a][h][:, c : c + n],
+                    start=(a == 0),
+                    stop=(a == 1),
+                )
+            bent = raw[:, (step % 3) * HALF : (step % 3) * HALF + n]
+            prod = raw[:, (3 + step % 3) * HALF : (3 + step % 3) * HALF + n]
+            nc.scalar.activation(out=bent, in_=bank, func=ACT.Tanh, scale=bend_sb[:, i : i + 1])
+            nc.vector.tensor_tensor(out=prod, in0=bank, in1=bent, op=MULT)
+
+        def put_y(i, c0, n, step):
+            prod = raw[:, (3 + step % 3) * HALF : (3 + step % 3) * HALF + n]
+            y = x_of(i, c0, n)
+            if step < 3:
+                nc.vector.tensor_tensor(out=y, in0=prod, in1=y, op=ADD)
+            else:
+                turned = raw[:, (6 + step % 2) * HALF : (7 + step % 2) * HALF]
+                add_on_tensor(y, y, prod, turned, step)
+            nc.vector.tensor_tensor(
+                out=page[i][:].indirect(listed(l_put2, c0, n)),
+                in0=y,
+                in1=wg[i % PACK][:, c0 : c0 + n],
+                op=MULT,
+            )
+
+        nc.vector.memset(s2raw[:].bitcast(I32), 0)
+        nc.vector.memset(tabs[:].bitcast(I32), 0)
+        make_identity(nc, ident[:])
+        nc.sync.dma_start(l_tab[:], offs)
+        load_w1(0, 0)
+        load_w1(0, 1)
+        load_tab(0)
+        for q in range(4):
+            nc.sync.dma_start(
+                out=s2raw[32 * q : 32 * q + 4, :].bitcast(I32).rearrange("p (a n) -> p a n", a=2),
+                in_=w2_scales[:, 4 * q : 4 * q + 4, :].rearrange("a r n -> r a n").bitcast(I32),
+            )
+        for q in range(4):
+            nc.sync.dma_start(
+                out=tabs[32 * q : 32 * q + 8, :].bitcast(I32),
+                in_=tab_scales[:, 4 * q : 4 * q + 4, :].bitcast(I32),
+            )
+        load_tab(1)
+        nc.sync.dma_start(l_put1[:], offs2)
+        nc.sync.dma_start(out=h_of(0), in_=rows(base, 0))
+        load_dealt(wgs_of(0), wgs, 0)
+        load_page(0)
+        nc.sync.dma_start(l_get[:], offs3)
+        nc.sync.dma_start(out=h_of(1), in_=rows(base, 1))
+        load_dealt(wgs_of(1), wgs, 1)
+        load_page(1)
+
+        nc.vector.tensor_copy(
+            out=s2p[:].rearrange("p (g t q) -> p g t q", t=PACK, q=P),
+            in_=s2raw[:].rearrange("p (g q t) -> p g t q", t=PACK, q=P),
+        )
+        for a in range(2):
+            quantise_w1(0, a)
+        for h in range(2):
+            nc.vector.tensor_copy(out=vw[0][h][:], in_=tabw[0][:].indirect(listed(l_tab, h * HALF, HALF)))
+        for h in range(2):
+            nc.vector.tensor_copy(out=vs[h][:], in_=tabs[:].indirect(listed(l_tab, h * HALF, HALF)))
+        for h in range(2):
+            nc.vector.tensor_copy(out=vw[1][h][:], in_=tabw[1][:].indirect(listed(l_tab, h * HALF, HALF)))
+
+        nc.sync.dma_start(out=h_of(2), in_=rows(base, 2))
+        for a in range(2):
+            load_w1(1, a)
+        nc.sync.dma_start(out=h_of(3), in_=rows(base, 3))
+        load_dealt(wgs_of(2), wgs, 2)
+        load_page(2)
+        load_dealt(wgs_of(3), wgs, 3)
+        load_page(3)
+        for i in range(4, TILES):
+            nc.sync.dma_start(out=h_of(i), in_=rows(base, i))
+        for i in range(4, TILES):
+            load_page(i)
+        nc.sync.dma_start(
+            out=w2raw[:].bitcast(I32).rearrange("p (a n) -> p a n", a=2),
+            in_=w2_words.rearrange("a p n -> p a n").bitcast(I32),
+        )
+        nc.sync.dma_start(
+            out=bend_sb[:].rearrange("p (b t) -> p b t", b=2),
+            in_=bend.rearrange("(b p t) -> p b t", b=2, t=PACK),
+        )
+        nc.sync.dma_start(l_put2[:], offs4)
+        load_dealt(wg[3][:], wgo, 3)
+
+        for i in range(TILES):
+            if i == 2:
+                for a in range(2):
+                    quantise_w1(1, a)
+            for h in range(2):
+                make_h(i, h)
+            put_h(i, 0, S)
+            if i < PACK:
+                get_x(i, 0, S)
+            elif i < TILES - 1:
+                get_x(i, 0, HALF)
+                load_dealt(wg[i - PACK][:], wgo, i - PACK)
+            else:
+                get_x(i, 0, HALF // 2)
+                get_x(i, HALF // 2, HALF // 2)
+
+        nc.scalar.copy(
+            out=w2p[:].bitcast(U16).rearrange("p (g t q) -> p g t q", t=PACK, q=P),
+            in_=w2raw[:].bitcast(U16).rearrange("p (g q t) -> p g t q", t=PACK, q=P),
+        )
+        quantise_abs(0, 0, HALF)
+        quantise_abs(0, HALF, HALF)
+        quantise_abs(1, 0, HALF // 2)
+        quantise_abs(1, HALF // 2, HALF // 2)
+        for i in range(PACK, TILES):
+            get_x(i, HALF, HALF)
+
+        pieces = [(0, 0, HALF // 2), (0, HALF // 2, HALF // 2)]
+        pieces += [(i, 0, HALF) for i in range(1, TILES)]
+        pieces += [(i, HALF, HALF) for i in range(TILES)]
+        make_product(*pieces[0], 0)
+        for step, (i, c0, n) in enumerate(pieces):
+            if step == 0:
+                put_y(i, c0, n, step)
+                make_product(*pieces[1], 1)
+            if step == 2:
+                quantise_abs(1, HALF, HALF)
+            if step + 2 < len(pieces):
+                make_product(*pieces[step + 2], step + 2)
+            if step > 0:
+                put_y(i, c0, n, step)
+            if c0 == HALF:
+                nc.sync.dma_start(out=rows(out, i), in_=page[i][:])

@@ -20,9 +20,11 @@ MULT = mybir.AluOpType.mult
 
 P = 128
 PACK = 4
-GROUP = P * PACK
+PASS = P * PACK
 HALF = 512
+QUARTER = 256
 TILES = 8
+LAST = TILES - 1
 
 
 def tile_list_etcher_drift_page_kernel(
@@ -43,66 +45,64 @@ def tile_list_etcher_drift_page_kernel(
         l_put2 = sb.tile([P, S // 16], U16, name="l_put2")
 
         page = [sbuf("page%d" % i, T2, F32) for i in range(TILES)]
-        hx = [sbuf("hx%d" % b, PACK * S, F32) for b in range(2)]
-        late = sbuf("late", 2 * S, F32)
-        wg = [sbuf("wg%d" % t, S, F32) for t in range(PACK)]
+        held = [sbuf("held%d" % i, S, F32) for i in range(TILES)]
+        sums = [sbuf("sums%d" % n, S, F32) for n in range(3)]
+        weighted = [sbuf("weighted%d" % n, S, F32) for n in range(3)]
+        wgs_sb = sbuf("wgs_sb", S, F32)
+        wgo_sb = sbuf("wgo_sb", S, F32)
         tabw = [sbuf("tabw%d" % a, T, U32) for a in range(2)]
         tabs = sbuf("tabs", T, U8)
         vw = [[sbuf("vw%d%d" % (a, h), HALF, U32) for h in range(2)] for a in range(2)]
         vs = [sbuf("vs%d" % h, HALF, U8) for h in range(2)]
-        raw = sbuf("raw", 2 * PACK * GROUP, F32)
-        grouped = [sbuf("grouped%d" % a, PACK * GROUP, BF16) for a in range(2)]
-        codes = [[sbuf("codes%d%d" % (b, a), GROUP, U32) for a in range(2)] for b in range(2)]
-        scales = [[sbuf("scales%d%d" % (b, a), GROUP, U8) for a in range(2)] for b in range(2)]
-        w2raw = sbuf("w2raw", 4 * H, U8)
-        w2p = sbuf("w2p", 4 * H, U8)
-        s2raw = sbuf("s2raw", 2 * H, U8)
-        s2p = sbuf("s2p", 2 * H, U8)
-        stage = [sbuf("stage%d" % n, S, F32) for n in range(2)]
+        raw = sbuf("raw", 2 * PACK * HALF, F32)
+        grouped = [sbuf("grouped%d" % a, S, F32) for a in range(2)]
+        codes = [sbuf("codes%d" % a, S, U32) for a in range(2)]
+        scales = [sbuf("scales%d" % a, S, U8) for a in range(2)]
+        turned = [[sbuf("turned%d%d" % (a, q), 2 * PASS, BF16) for q in range(4)] for a in range(2)]
+        w2w = sbuf("w2w", 4 * H, U8)
+        w2s = sbuf("w2s", 2 * H, U8)
         ident = sbuf("ident", P, F32)
         bend_sb = sbuf("bend_sb", TILES, F32)
 
         mm_banks = [ps.tile([P, HALF], F32, name="mm%d" % n) for n in range(4)]
-        sum_banks = [ps.tile([P, HALF], F32, name="sum%d" % n) for n in range(2)]
-        back_banks = [ps.tile([P, HALF], F32, name="back%d" % n) for n in range(2)]
+        x_banks = [ps.tile([P, HALF], F32, name="xb%d" % n) for n in range(2)]
+        word_banks = [ps.tile([P, HALF], F32, name="wb%d" % n) for n in range(2)]
 
         def rows(dram, i):
-            b, t = divmod(i, PACK)
-            return dram.rearrange("(b p t) c -> b t p c", b=2, t=PACK)[b, t]
+            return dram[i * P : (i + 1) * P, :]
 
         def listed(lst, c0, n):
             return lst[:, c0 // 16 : (c0 + n) // 16]
 
-        def h_of(i):
-            b, t = divmod(i, PACK)
-            return late[:, S : 2 * S] if i == TILES - 1 else hx[b][:, t * S : (t + 1) * S]
-
-        def wgs_of(t):
-            return late[:, 0:S] if t == PACK - 1 else wg[t][:]
-
-        def x_planes(b, h):
-            if b == 1 and h == 1:
-                return late[:].rearrange("p (t c) -> p t c", t=PACK)
-            return hx[b][:].rearrange("p (t c) -> p t c", t=PACK)[:, :, h * HALF : (h + 1) * HALF]
+        def base_of(i):
+            return held[(i - 1) % TILES]
 
         def x_of(i, c0, n):
-            b, t = divmod(i, PACK)
-            h, c = divmod(c0, HALF)
-            if b == 1 and h == 1:
-                return late[:, t * HALF + c : t * HALF + c + n]
-            return hx[b][:, t * S + c0 : t * S + c0 + n]
+            if i >= 4 and c0 >= HALF:
+                home = weighted[LAST % 3] if i < 6 else grouped[0]
+                c = (i % 2) * HALF + c0 - HALF
+                return home[:, c : c + n]
+            return held[i][:, c0 : c0 + n]
 
-        def load_dealt(dst, src, t):
-            picked = src.rearrange("(q t) j -> t q j", t=PACK)[t]
-            for c in range(4):
-                nc.sync.dma_start(out=dst[32 * c : 32 * (c + 1), :], in_=picked)
+        def w1_raw(a, c0, n):
+            r0 = PACK * (a * HALF + c0 % HALF)
+            return raw[:, r0 : r0 + PACK * n]
 
-        def load_w1(b, a):
-            src = w1[a * GROUP : (a + 1) * GROUP, b * GROUP : (b + 1) * GROUP]
-            dst = raw[:, a * PACK * GROUP : (a + 1) * PACK * GROUP]
+        def load_w1(a, c0, n):
             nc.sync.dma_start(
-                out=dst.rearrange("p (j c) -> p j c", j=PACK),
-                in_=src.rearrange("(p j) c -> p j c", j=PACK),
+                out=w1_raw(a, c0, n).rearrange("p (j c) -> p j c", j=PACK),
+                in_=w1[a * PASS : (a + 1) * PASS, c0 : c0 + n].rearrange("(p j) c -> p j c", j=PACK),
+            )
+
+        def quantise_w1(a, c0, n):
+            g0 = PACK * (c0 % HALF)
+            rounded = grouped[a][:].bitcast(BF16)[:, g0 : g0 + PACK * n]
+            nc.scalar.copy(
+                out=rounded.rearrange("p (c j) -> p c j", j=PACK),
+                in_=w1_raw(a, c0, n).rearrange("p (j c) -> p c j", j=PACK),
+            )
+            nc.vector.quantize_mx(
+                out=codes[a][:, c0 : c0 + n].bitcast(FP8X4), scales=scales[a][:, c0 : c0 + n], in_=rounded
             )
 
         def load_tab(a):
@@ -111,207 +111,196 @@ def tile_list_etcher_drift_page_kernel(
                 in_=tab_words[a].rearrange("p n t -> p (n t)").bitcast(I32),
             )
 
-        def load_page(i):
+        def load_tile(i):
+            nc.sync.dma_start(out=base_of(i)[:], in_=rows(base, i))
             nc.sync.dma_start(out=page[i][:], in_=rows(page0, i))
 
-        def quantise_w1(b, a):
-            src = raw[:, a * PACK * GROUP : (a + 1) * PACK * GROUP]
-            nc.scalar.copy(
-                out=grouped[a][:].rearrange("p (t m j) -> p m t j", t=PACK, j=PACK),
-                in_=src.rearrange("p (j m t) -> p m t j", j=PACK, t=PACK),
-            )
-            nc.vector.quantize_mx(
-                out=codes[b][a][:].bitcast(FP8X4), scales=scales[b][a][:], in_=grouped[a][:]
-            )
-
-        def add_on_tensor(dst, first, second, turned, step):
-            sum_bank, back_bank = sum_banks[step % 2], back_banks[step % 2]
-            for q in range(HALF // P):
-                blk = slice(q * P, (q + 1) * P)
-                nc.tensor.matmul(sum_bank[:, blk], lhsT=first[:, blk], rhs=ident[:],
-                                 is_transpose=True, start=True, stop=False)
-                nc.tensor.matmul(sum_bank[:, blk], lhsT=second[:, blk], rhs=ident[:],
-                                 is_transpose=True, start=False, stop=True)
-            nc.scalar.copy(out=turned, in_=sum_bank[:])
-            for q in range(HALF // P):
-                blk = slice(q * P, (q + 1) * P)
-                nc.tensor.transpose(back_bank[:, blk], turned[:, blk], ident[:])
-            nc.scalar.copy(out=dst, in_=back_bank[:])
-
-        def make_h(i, h):
-            b, t = divmod(i, PACK)
-            step = 2 * i + h
-            bank = mm_banks[step % 4]
-            cols = slice(t * P, (t + 1) * P)
+        def first_product(i, h):
+            bank = mm_banks[(2 * i + h) % 4]
+            cols = slice(i * P, (i + 1) * P)
             for a in range(2):
                 nc.tensor.matmul_mx(
                     out=bank[:],
-                    lhsT=codes[b][a][:, cols].bitcast(FP8X4),
-                    lhsT_scale=scales[b][a][:, cols],
+                    lhsT=codes[a][:, cols].bitcast(FP8X4),
+                    lhsT_scale=scales[a][:, cols],
                     rhs=vw[a][h][:].bitcast(FP8X4),
                     rhs_scale=vs[h][4 * a : P, :],
                     start=(a == 0),
                     stop=(a == 1),
                 )
-            dst = h_of(i)[:, h * HALF : (h + 1) * HALF]
-            if i == 0:
-                nc.vector.tensor_tensor(out=dst, in0=bank[:], in1=dst, op=ADD)
-            else:
-                slot = slice((step % 2) * HALF, (step % 2 + 1) * HALF)
-                nc.scalar.copy(out=stage[0][:, slot], in_=bank[:])
-                add_on_tensor(dst, dst, stage[0][:, slot], stage[1][:, slot], step)
+            return bank
+
+        def weigh_h(i, c0, n):
+            cols = slice(c0, c0 + n)
+            h_sb = base_of(i)[:, cols]
+            nc.gpsimd.tensor_tensor(out=h_sb, in0=h_sb, in1=sums[i % 3][:, cols], op=ADD)
+            nc.gpsimd.tensor_tensor(out=weighted[i % 3][:, cols], in0=h_sb, in1=wgs_sb[:, cols], op=MULT)
 
         def put_h(i, c0, n):
-            nc.vector.tensor_tensor(
-                out=page[i][:].indirect(listed(l_put1, c0, n)),
-                in0=h_of(i)[:, c0 : c0 + n],
-                in1=wgs_of(i % PACK)[:, c0 : c0 + n],
-                op=MULT,
+            nc.vector.tensor_copy(
+                out=page[i][:].indirect(listed(l_put1, c0, n)), in_=weighted[i % 3][:, c0 : c0 + n]
             )
 
         def get_x(i, c0, n):
             nc.vector.tensor_copy(out=x_of(i, c0, n), in_=page[i][:].indirect(listed(l_get, c0, n)))
 
-        def quantise_abs(b, c0, n):
+        def turn_x(i, c0, n, turn):
+            a, part = divmod(i, PACK)
+            bank = x_banks[turn % 2]
+            x = x_of(i, c0, n)
+            for blk in range(n // P):
+                cols = slice(blk * P, (blk + 1) * P)
+                nc.tensor.transpose(bank[:, cols], x[:, cols], ident[:])
+            for q in range(n // QUARTER):
+                dst = turned[a][c0 // QUARTER + q][:].rearrange("p (blk m) -> p blk m", blk=2)
+                nc.scalar.activation(
+                    out=dst[:, :, part * P : (part + 1) * P],
+                    in_=bank[:, q * QUARTER : (q + 1) * QUARTER].rearrange("p (blk m) -> p blk m", blk=2),
+                    func=ACT.Abs,
+                )
+
+        def quantise_abs(a, c0, n):
             h, c = divmod(c0, HALF)
-            mags = stage[h][:].bitcast(BF16) if b == 0 else grouped[h][:]
-            mags = mags[:, PACK * c : PACK * (c + n)]
-            nc.scalar.activation(
-                out=mags.rearrange("p (c t) -> p c t", t=PACK),
-                in_=x_planes(b, h)[:, :, c : c + n].rearrange("p t c -> p c t"),
-                func=ACT.Abs,
-            )
+            home = grouped[h] if a == 1 else weighted[(5 + h) % 3]
+            for q in range(c0 // QUARTER, (c0 + n) // QUARTER):
+                bank = word_banks[q % 2]
+                words = turned[a][q][:].bitcast(F32)
+                for blk in range(2):
+                    for u in range(2):
+                        col = (2 * blk + u) * P
+                        nc.tensor.transpose(
+                            bank[:, col : col + P],
+                            words[:, blk * QUARTER + u : (blk + 1) * QUARTER : 2],
+                            ident[:],
+                        )
+                dst = home[:, (q % 2) * HALF : (q % 2 + 1) * HALF]
+                nc.scalar.copy(
+                    out=dst.rearrange("p (blk j u) -> p blk j u", blk=2, u=2),
+                    in_=bank[:].rearrange("p (blk u j) -> p blk j u", blk=2, u=2),
+                )
             nc.vector.quantize_mx(
-                out=codes[b][h][:, c : c + n].bitcast(FP8X4),
-                scales=scales[b][h][:, c : c + n],
-                in_=mags,
+                out=codes[a][:, c0 : c0 + n].bitcast(FP8X4),
+                scales=scales[a][:, c0 : c0 + n],
+                in_=home[:].bitcast(BF16)[:, PACK * c : PACK * (c + n)],
             )
 
+        def slot(k, n):
+            return raw[:, k * HALF : k * HALF + n]
+
         def make_product(i, c0, n, step):
-            h, c = divmod(c0, HALF)
             bank = mm_banks[step % 4][:, 0:n]
             for a in range(2):
                 col = a * H + i * P
                 nc.tensor.matmul_mx(
                     out=bank,
-                    lhsT=w2p[:, 2 * col : 2 * (col + P)].bitcast(FP4X4),
-                    lhsT_scale=s2p[:, col : col + P],
-                    rhs=codes[a][h][:, c : c + n].bitcast(FP8X4),
-                    rhs_scale=scales[a][h][:, c : c + n],
+                    lhsT=w2w[:, 2 * col : 2 * (col + P)].bitcast(FP4X4),
+                    lhsT_scale=w2s[:, col : col + P],
+                    rhs=codes[a][:, c0 : c0 + n].bitcast(FP8X4),
+                    rhs_scale=scales[a][:, c0 : c0 + n],
                     start=(a == 0),
                     stop=(a == 1),
                 )
-            bent = raw[:, (step % 3) * HALF : (step % 3) * HALF + n]
-            prod = raw[:, (3 + step % 3) * HALF : (3 + step % 3) * HALF + n]
+            bent, prod = slot(step % 4, n), slot(4 + step % 4, n)
             nc.scalar.activation(out=bent, in_=bank, func=ACT.Tanh, scale=bend_sb[:, i : i + 1])
-            nc.vector.tensor_tensor(out=prod, in0=bank, in1=bent, op=MULT)
+            if step < 3 or step % 2 == 0:
+                nc.vector.tensor_tensor(out=prod, in0=bank, in1=bent, op=MULT)
+            else:
+                nc.scalar.copy(out=prod, in_=bank)
+                nc.gpsimd.tensor_tensor(out=prod, in0=prod, in1=bent, op=MULT)
 
         def put_y(i, c0, n, step):
-            prod = raw[:, (3 + step % 3) * HALF : (3 + step % 3) * HALF + n]
             y = x_of(i, c0, n)
-            if step < 3:
-                nc.vector.tensor_tensor(out=y, in0=prod, in1=y, op=ADD)
-            else:
-                turned = raw[:, (6 + step % 2) * HALF : (7 + step % 2) * HALF]
-                add_on_tensor(y, y, prod, turned, step)
-            nc.vector.tensor_tensor(
-                out=page[i][:].indirect(listed(l_put2, c0, n)),
-                in0=y,
-                in1=wg[i % PACK][:, c0 : c0 + n],
-                op=MULT,
-            )
+            engine = nc.vector if step < 2 else nc.gpsimd
+            engine.tensor_tensor(out=y, in0=slot(4 + step % 4, n), in1=y, op=ADD)
+            engine.tensor_tensor(out=y, in0=y, in1=wgo_sb[:, c0 : c0 + n], op=MULT)
+            nc.vector.tensor_copy(out=page[i][:].indirect(listed(l_put2, c0, n)), in_=y)
 
-        nc.vector.memset(s2raw[:].bitcast(I32), 0)
         nc.vector.memset(tabs[:].bitcast(I32), 0)
+        nc.vector.memset(w2s[:].bitcast(I32), 0)
         make_identity(nc, ident[:])
         nc.sync.dma_start(l_tab[:], offs)
-        load_w1(0, 0)
-        load_w1(0, 1)
         load_tab(0)
         for q in range(4):
-            nc.sync.dma_start(
-                out=s2raw[32 * q : 32 * q + 4, :].bitcast(I32).rearrange("p (a n) -> p a n", a=2),
-                in_=w2_scales[:, 4 * q : 4 * q + 4, :].rearrange("a r n -> r a n").bitcast(I32),
-            )
-        for q in range(4):
-            nc.sync.dma_start(
+            nc.scalar.dma_start(
                 out=tabs[32 * q : 32 * q + 8, :].bitcast(I32),
                 in_=tab_scales[:, 4 * q : 4 * q + 4, :].bitcast(I32),
             )
+        for a in range(2):
+            load_w1(a, 0, QUARTER)
         load_tab(1)
+        nc.sync.dma_start(out=wgs_sb[:], in_=wgs)
         nc.sync.dma_start(l_put1[:], offs2)
-        nc.sync.dma_start(out=h_of(0), in_=rows(base, 0))
-        load_dealt(wgs_of(0), wgs, 0)
-        load_page(0)
+        load_tile(0)
+        nc.sync.dma_start(out=base_of(1)[:], in_=rows(base, 1))
+        for a in range(2):
+            load_w1(a, QUARTER, QUARTER)
+        nc.sync.dma_start(out=page[1][:], in_=rows(page0, 1))
         nc.sync.dma_start(l_get[:], offs3)
-        nc.sync.dma_start(out=h_of(1), in_=rows(base, 1))
-        load_dealt(wgs_of(1), wgs, 1)
-        load_page(1)
+        load_tile(2)
 
-        nc.vector.tensor_copy(
-            out=s2p[:].rearrange("p (g t q) -> p g t q", t=PACK, q=P),
-            in_=s2raw[:].rearrange("p (g q t) -> p g t q", t=PACK, q=P),
-        )
         for a in range(2):
-            quantise_w1(0, a)
-        for h in range(2):
-            nc.vector.tensor_copy(out=vw[0][h][:], in_=tabw[0][:].indirect(listed(l_tab, h * HALF, HALF)))
-        for h in range(2):
-            nc.vector.tensor_copy(out=vs[h][:], in_=tabs[:].indirect(listed(l_tab, h * HALF, HALF)))
-        for h in range(2):
-            nc.vector.tensor_copy(out=vw[1][h][:], in_=tabw[1][:].indirect(listed(l_tab, h * HALF, HALF)))
+            quantise_w1(a, 0, QUARTER)
+        for window, picked in ((tabs, vs), (tabw[0], vw[0]), (tabw[1], vw[1])):
+            for h in range(2):
+                nc.vector.tensor_copy(out=picked[h][:], in_=window[:].indirect(listed(l_tab, h * HALF, HALF)))
 
-        nc.sync.dma_start(out=h_of(2), in_=rows(base, 2))
+        bank = first_product(0, 0)
+        h_sb = base_of(0)[:, 0:HALF]
+        nc.vector.tensor_tensor(out=h_sb, in0=bank[:], in1=h_sb, op=ADD)
+        nc.vector.tensor_tensor(out=weighted[0][:, 0:HALF], in0=h_sb, in1=wgs_sb[:, 0:HALF], op=MULT)
+        nc.scalar.copy(out=sums[0][:, HALF:S], in_=first_product(0, 1)[:])
+        weigh_h(0, HALF, HALF)
         for a in range(2):
-            load_w1(1, a)
-        nc.sync.dma_start(out=h_of(3), in_=rows(base, 3))
-        load_dealt(wgs_of(2), wgs, 2)
-        load_page(2)
-        load_dealt(wgs_of(3), wgs, 3)
-        load_page(3)
-        for i in range(4, TILES):
-            nc.sync.dma_start(out=h_of(i), in_=rows(base, i))
-        for i in range(4, TILES):
-            load_page(i)
+            quantise_w1(a, QUARTER, QUARTER)
+        put_h(0, 0, HALF)
+        put_h(0, HALF, HALF)
+
+        for a in range(2):
+            load_w1(a, HALF, HALF)
+        load_tile(3)
         nc.sync.dma_start(
-            out=w2raw[:].bitcast(I32).rearrange("p (a n) -> p a n", a=2),
+            out=w2w[:].bitcast(I32).rearrange("p (a n) -> p a n", a=2),
             in_=w2_words.rearrange("a p n -> p a n").bitcast(I32),
         )
-        nc.sync.dma_start(
-            out=bend_sb[:].rearrange("p (b t) -> p b t", b=2),
-            in_=bend.rearrange("(b p t) -> p b t", b=2, t=PACK),
-        )
+        for q in range(4):
+            nc.sync.dma_start(
+                out=w2s[32 * q : 32 * q + 4, :].bitcast(I32).rearrange("p (a n) -> p a n", a=2),
+                in_=w2_scales[:, 4 * q : 4 * q + 4, :].rearrange("a r n -> r a n").bitcast(I32),
+            )
+        with nc.allow_non_contiguous_dma(reason="one bend value a partition and tile"):
+            nc.sync.dma_start(out=bend_sb[:], in_=bend.rearrange("(i p) -> p i", p=P))
         nc.sync.dma_start(l_put2[:], offs4)
-        load_dealt(wg[3][:], wgo, 3)
+        nc.sync.dma_start(out=wgo_sb[:], in_=wgo)
+        for i in range(4, TILES):
+            load_tile(i)
 
-        for i in range(TILES):
+        for i in range(1, TILES):
             if i == 2:
                 for a in range(2):
-                    quantise_w1(1, a)
+                    quantise_w1(a, HALF, HALF)
             for h in range(2):
-                make_h(i, h)
+                nc.scalar.copy(out=sums[i % 3][:, h * HALF : (h + 1) * HALF], in_=first_product(i, h)[:])
+            weigh_h(i, 0, S)
             put_h(i, 0, S)
-            if i < PACK:
-                get_x(i, 0, S)
-            elif i < TILES - 1:
-                get_x(i, 0, HALF)
-                load_dealt(wg[i - PACK][:], wgo, i - PACK)
+            if i <= 4:
+                get_x(i - 1, 0, S)
+                turn_x(i - 1, 0, HALF, 0)
+                turn_x(i - 1, HALF, HALF, 1)
             else:
-                get_x(i, 0, HALF // 2)
-                get_x(i, HALF // 2, HALF // 2)
-
-        nc.scalar.copy(
-            out=w2p[:].bitcast(U16).rearrange("p (g t q) -> p g t q", t=PACK, q=P),
-            in_=w2raw[:].bitcast(U16).rearrange("p (g q t) -> p g t q", t=PACK, q=P),
-        )
-        quantise_abs(0, 0, HALF)
+                get_x(i - 1, 0, HALF)
+                turn_x(i - 1, 0, HALF, i)
+            if i == 5:
+                quantise_abs(0, 0, HALF)
         quantise_abs(0, HALF, HALF)
-        quantise_abs(1, 0, HALF // 2)
-        quantise_abs(1, HALF // 2, HALF // 2)
-        for i in range(PACK, TILES):
+        for q in range(2):
+            get_x(LAST, q * QUARTER, QUARTER)
+        for q in range(2):
+            turn_x(LAST, q * QUARTER, QUARTER, q)
+            quantise_abs(1, q * QUARTER, QUARTER)
+        for i in range(4, TILES):
             get_x(i, HALF, HALF)
 
-        pieces = [(0, 0, HALF // 2), (0, HALF // 2, HALF // 2)]
+        pieces = [(0, 0, QUARTER), (0, QUARTER, QUARTER)]
         pieces += [(i, 0, HALF) for i in range(1, TILES)]
         pieces += [(i, HALF, HALF) for i in range(TILES)]
         make_product(*pieces[0], 0)
@@ -320,6 +309,8 @@ def tile_list_etcher_drift_page_kernel(
                 put_y(i, c0, n, step)
                 make_product(*pieces[1], 1)
             if step == 2:
+                for late in range(4, TILES):
+                    turn_x(late, HALF, HALF, late)
                 quantise_abs(1, HALF, HALF)
             if step + 2 < len(pieces):
                 make_product(*pieces[step + 2], step + 2)

from contextlib import ExitStack

import concourse.mybir as mybir
from concourse.masks import make_identity

K, T, S, H, T2 = 1024, 4096, 1024, 1024, 2048
FLOPS = 2 * K * H * S + 2 * H * H * S

F32 = mybir.dt.float32
BF16 = mybir.dt.bfloat16
I32 = mybir.dt.int32
U32 = mybir.dt.uint32
U16 = mybir.dt.uint16
U8 = mybir.dt.uint8
FP8X4 = mybir.dt.float8_e4m3fn_x4
FP4X4 = mybir.dt.float4_e2m1fn_x4
ACT = mybir.ActivationFunctionType
ADD = mybir.AluOpType.add
MULT = mybir.AluOpType.mult

P = 128
PACK = 4
PASS = P * PACK
HALF = 512
QUARTER = 256
TILES = 8
LAST = TILES - 1


def tile_list_etcher_drift_page_kernel(
    tc, tab_words, tab_scales, offs, w1, base, page0, wgs, offs2, offs3,
    w2_words, w2_scales, bend, wgo, offs4, out,
):
    nc = tc.nc
    with ExitStack() as ctx:
        sb = ctx.enter_context(tc.tile_pool(name="sb", bufs=1))
        ps = ctx.enter_context(tc.psum_pool(name="ps", bufs=1))

        def sbuf(name, cols, dtype):
            return sb.tile([P, cols], dtype, name=name, align_bytes=64)

        l_tab = sb.tile([P, S // 16], U16, name="l_tab")
        l_put1 = sb.tile([P, S // 16], U16, name="l_put1")
        l_get = sb.tile([P, S // 16], U16, name="l_get")
        l_put2 = sb.tile([P, S // 16], U16, name="l_put2")

        page = [sbuf("page%d" % i, T2, F32) for i in range(TILES)]
        held = [sbuf("held%d" % i, S, F32) for i in range(TILES)]
        sums = [sbuf("sums%d" % n, S, F32) for n in range(3)]
        weighted = [sbuf("weighted%d" % n, S, F32) for n in range(3)]
        wgs_sb = sbuf("wgs_sb", S, F32)
        wgo_sb = sbuf("wgo_sb", S, F32)
        tabw = [sbuf("tabw%d" % a, T, U32) for a in range(2)]
        tabs = sbuf("tabs", T, U8)
        vw = [[sbuf("vw%d%d" % (a, h), HALF, U32) for h in range(2)] for a in range(2)]
        vs = [sbuf("vs%d" % h, HALF, U8) for h in range(2)]
        raw = sbuf("raw", 2 * PACK * HALF, F32)
        grouped = [sbuf("grouped%d" % a, S, F32) for a in range(2)]
        codes = [sbuf("codes%d" % a, S, U32) for a in range(2)]
        scales = [sbuf("scales%d" % a, S, U8) for a in range(2)]
        turned = [[sbuf("turned%d%d" % (a, q), 2 * PASS, BF16) for q in range(4)] for a in range(2)]
        w2w = sbuf("w2w", 4 * H, U8)
        w2s = sbuf("w2s", 2 * H, U8)
        ident = sbuf("ident", P, F32)
        bend_sb = sbuf("bend_sb", TILES, F32)

        mm_banks = [ps.tile([P, HALF], F32, name="mm%d" % n) for n in range(4)]
        x_banks = [ps.tile([P, HALF], F32, name="xb%d" % n) for n in range(2)]
        word_banks = [ps.tile([P, HALF], F32, name="wb%d" % n) for n in range(2)]

        def rows(dram, i):
            return dram[i * P : (i + 1) * P, :]

        def listed(lst, c0, n):
            return lst[:, c0 // 16 : (c0 + n) // 16]

        def base_of(i):
            return held[(i - 1) % TILES]

        def x_of(i, c0, n):
            if i >= 4 and c0 >= HALF:
                home = weighted[LAST % 3] if i < 6 else grouped[0]
                c = (i % 2) * HALF + c0 - HALF
                return home[:, c : c + n]
            return held[i][:, c0 : c0 + n]

        def w1_raw(a, c0, n):
            r0 = PACK * (a * HALF + c0 % HALF)
            return raw[:, r0 : r0 + PACK * n]

        def load_w1(a, c0, n):
            nc.sync.dma_start(
                out=w1_raw(a, c0, n).rearrange("p (j c) -> p j c", j=PACK),
                in_=w1[a * PASS : (a + 1) * PASS, c0 : c0 + n].rearrange("(p j) c -> p j c", j=PACK),
            )

        def quantise_w1(a, c0, n):
            g0 = PACK * (c0 % HALF)
            rounded = grouped[a][:].bitcast(BF16)[:, g0 : g0 + PACK * n]
            nc.scalar.copy(
                out=rounded.rearrange("p (c j) -> p c j", j=PACK),
                in_=w1_raw(a, c0, n).rearrange("p (j c) -> p c j", j=PACK),
            )
            nc.vector.quantize_mx(
                out=codes[a][:, c0 : c0 + n].bitcast(FP8X4), scales=scales[a][:, c0 : c0 + n], in_=rounded
            )

        def load_tab(a):
            nc.sync.dma_start(
                out=tabw[a][:].bitcast(I32),
                in_=tab_words[a].rearrange("p n t -> p (n t)").bitcast(I32),
            )

        def load_tile(i):
            nc.sync.dma_start(out=base_of(i)[:], in_=rows(base, i))
            nc.sync.dma_start(out=page[i][:], in_=rows(page0, i))

        def first_product(i, h):
            bank = mm_banks[(2 * i + h) % 4]
            cols = slice(i * P, (i + 1) * P)
            for a in range(2):
                nc.tensor.matmul_mx(
                    out=bank[:],
                    lhsT=codes[a][:, cols].bitcast(FP8X4),
                    lhsT_scale=scales[a][:, cols],
                    rhs=vw[a][h][:].bitcast(FP8X4),
                    rhs_scale=vs[h][4 * a : P, :],
                    start=(a == 0),
                    stop=(a == 1),
                )
            return bank

        def weigh_h(i, c0, n):
            cols = slice(c0, c0 + n)
            h_sb = base_of(i)[:, cols]
            nc.gpsimd.tensor_tensor(out=h_sb, in0=h_sb, in1=sums[i % 3][:, cols], op=ADD)
            nc.gpsimd.tensor_tensor(out=weighted[i % 3][:, cols], in0=h_sb, in1=wgs_sb[:, cols], op=MULT)

        def put_h(i, c0, n):
            nc.vector.tensor_copy(
                out=page[i][:].indirect(listed(l_put1, c0, n)), in_=weighted[i % 3][:, c0 : c0 + n]
            )

        def get_x(i, c0, n):
            nc.vector.tensor_copy(out=x_of(i, c0, n), in_=page[i][:].indirect(listed(l_get, c0, n)))

        def turn_x(i, c0, n, turn):
            a, part = divmod(i, PACK)
            bank = x_banks[turn % 2]
            x = x_of(i, c0, n)
            for blk in range(n // P):
                cols = slice(blk * P, (blk + 1) * P)
                nc.tensor.transpose(bank[:, cols], x[:, cols], ident[:])
            for q in range(n // QUARTER):
                dst = turned[a][c0 // QUARTER + q][:].rearrange("p (blk m) -> p blk m", blk=2)
                nc.scalar.activation(
                    out=dst[:, :, part * P : (part + 1) * P],
                    in_=bank[:, q * QUARTER : (q + 1) * QUARTER].rearrange("p (blk m) -> p blk m", blk=2),
                    func=ACT.Abs,
                )

        def quantise_abs(a, c0, n):
            h, c = divmod(c0, HALF)
            home = grouped[h] if a == 1 else weighted[(5 + h) % 3]
            for q in range(c0 // QUARTER, (c0 + n) // QUARTER):
                bank = word_banks[q % 2]
                words = turned[a][q][:].bitcast(F32)
                for blk in range(2):
                    for u in range(2):
                        col = (2 * blk + u) * P
                        nc.tensor.transpose(
                            bank[:, col : col + P],
                            words[:, blk * QUARTER + u : (blk + 1) * QUARTER : 2],
                            ident[:],
                        )
                dst = home[:, (q % 2) * HALF : (q % 2 + 1) * HALF]
                nc.scalar.copy(
                    out=dst.rearrange("p (blk j u) -> p blk j u", blk=2, u=2),
                    in_=bank[:].rearrange("p (blk u j) -> p blk j u", blk=2, u=2),
                )
            nc.vector.quantize_mx(
                out=codes[a][:, c0 : c0 + n].bitcast(FP8X4),
                scales=scales[a][:, c0 : c0 + n],
                in_=home[:].bitcast(BF16)[:, PACK * c : PACK * (c + n)],
            )

        def slot(k, n):
            return raw[:, k * HALF : k * HALF + n]

        def make_product(i, c0, n, step):
            bank = mm_banks[step % 4][:, 0:n]
            for a in range(2):
                col = a * H + i * P
                nc.tensor.matmul_mx(
                    out=bank,
                    lhsT=w2w[:, 2 * col : 2 * (col + P)].bitcast(FP4X4),
                    lhsT_scale=w2s[:, col : col + P],
                    rhs=codes[a][:, c0 : c0 + n].bitcast(FP8X4),
                    rhs_scale=scales[a][:, c0 : c0 + n],
                    start=(a == 0),
                    stop=(a == 1),
                )
            bent, prod = slot(step % 4, n), slot(4 + step % 4, n)
            nc.scalar.activation(out=bent, in_=bank, func=ACT.Tanh, scale=bend_sb[:, i : i + 1])
            if step < 3 or step % 2 == 0:
                nc.vector.tensor_tensor(out=prod, in0=bank, in1=bent, op=MULT)
            else:
                nc.scalar.copy(out=prod, in_=bank)
                nc.gpsimd.tensor_tensor(out=prod, in0=prod, in1=bent, op=MULT)

        def put_y(i, c0, n, step):
            y = x_of(i, c0, n)
            engine = nc.vector if step < 2 else nc.gpsimd
            engine.tensor_tensor(out=y, in0=slot(4 + step % 4, n), in1=y, op=ADD)
            engine.tensor_tensor(out=y, in0=y, in1=wgo_sb[:, c0 : c0 + n], op=MULT)
            nc.vector.tensor_copy(out=page[i][:].indirect(listed(l_put2, c0, n)), in_=y)

        nc.vector.memset(tabs[:].bitcast(I32), 0)
        nc.vector.memset(w2s[:].bitcast(I32), 0)
        make_identity(nc, ident[:])
        nc.sync.dma_start(l_tab[:], offs)
        load_tab(0)
        for q in range(4):
            nc.scalar.dma_start(
                out=tabs[32 * q : 32 * q + 8, :].bitcast(I32),
                in_=tab_scales[:, 4 * q : 4 * q + 4, :].bitcast(I32),
            )
        for a in range(2):
            load_w1(a, 0, QUARTER)
        load_tab(1)
        nc.sync.dma_start(out=wgs_sb[:], in_=wgs)
        nc.sync.dma_start(l_put1[:], offs2)
        load_tile(0)
        nc.sync.dma_start(out=base_of(1)[:], in_=rows(base, 1))
        for a in range(2):
            load_w1(a, QUARTER, QUARTER)
        nc.sync.dma_start(out=page[1][:], in_=rows(page0, 1))
        nc.sync.dma_start(l_get[:], offs3)
        load_tile(2)

        for a in range(2):
            quantise_w1(a, 0, QUARTER)
        for window, picked in ((tabs, vs), (tabw[0], vw[0]), (tabw[1], vw[1])):
            for h in range(2):
                nc.vector.tensor_copy(out=picked[h][:], in_=window[:].indirect(listed(l_tab, h * HALF, HALF)))

        bank = first_product(0, 0)
        h_sb = base_of(0)[:, 0:HALF]
        nc.vector.tensor_tensor(out=h_sb, in0=bank[:], in1=h_sb, op=ADD)
        nc.vector.tensor_tensor(out=weighted[0][:, 0:HALF], in0=h_sb, in1=wgs_sb[:, 0:HALF], op=MULT)
        nc.scalar.copy(out=sums[0][:, HALF:S], in_=first_product(0, 1)[:])
        weigh_h(0, HALF, HALF)
        for a in range(2):
            quantise_w1(a, QUARTER, QUARTER)
        put_h(0, 0, HALF)
        put_h(0, HALF, HALF)

        for a in range(2):
            load_w1(a, HALF, HALF)
        load_tile(3)
        nc.sync.dma_start(
            out=w2w[:].bitcast(I32).rearrange("p (a n) -> p a n", a=2),
            in_=w2_words.rearrange("a p n -> p a n").bitcast(I32),
        )
        for q in range(4):
            nc.sync.dma_start(
                out=w2s[32 * q : 32 * q + 4, :].bitcast(I32).rearrange("p (a n) -> p a n", a=2),
                in_=w2_scales[:, 4 * q : 4 * q + 4, :].rearrange("a r n -> r a n").bitcast(I32),
            )
        with nc.allow_non_contiguous_dma(reason="one bend value a partition and tile"):
            nc.sync.dma_start(out=bend_sb[:], in_=bend.rearrange("(i p) -> p i", p=P))
        nc.sync.dma_start(l_put2[:], offs4)
        nc.sync.dma_start(out=wgo_sb[:], in_=wgo)
        for i in range(4, TILES):
            load_tile(i)

        for i in range(1, TILES):
            if i == 2:
                for a in range(2):
                    quantise_w1(a, HALF, HALF)
            for h in range(2):
                nc.scalar.copy(out=sums[i % 3][:, h * HALF : (h + 1) * HALF], in_=first_product(i, h)[:])
            weigh_h(i, 0, S)
            put_h(i, 0, S)
            if i <= 4:
                get_x(i - 1, 0, S)
                turn_x(i - 1, 0, HALF, 0)
                turn_x(i - 1, HALF, HALF, 1)
            else:
                get_x(i - 1, 0, HALF)
                turn_x(i - 1, 0, HALF, i)
            if i == 5:
                quantise_abs(0, 0, HALF)
        quantise_abs(0, HALF, HALF)
        for q in range(2):
            get_x(LAST, q * QUARTER, QUARTER)
        for q in range(2):
            turn_x(LAST, q * QUARTER, QUARTER, q)
            quantise_abs(1, q * QUARTER, QUARTER)
        for i in range(4, TILES):
            get_x(i, HALF, HALF)

        pieces = [(0, 0, QUARTER), (0, QUARTER, QUARTER)]
        pieces += [(i, 0, HALF) for i in range(1, TILES)]
        pieces += [(i, HALF, HALF) for i in range(TILES)]
        make_product(*pieces[0], 0)
        for step, (i, c0, n) in enumerate(pieces):
            if step == 0:
                put_y(i, c0, n, step)
                make_product(*pieces[1], 1)
            if step == 2:
                for late in range(4, TILES):
                    turn_x(late, HALF, HALF, late)
                quantise_abs(1, HALF, HALF)
            if step + 2 < len(pieces):
                make_product(*pieces[step + 2], step + 2)
            if step > 0:
                put_y(i, c0, n, step)
            if c0 == HALF:
                nc.sync.dma_start(out=rows(out, i), in_=page[i][:])
